import numpy as np
import ml_dtypes


def mxq(x, axis, fmt="e4m3"):
    dtype, down = {"e4m3": (ml_dtypes.float8_e4m3fn, 7), "e5m2": (ml_dtypes.float8_e5m2, 14)}[fmt]
    v = np.moveaxis(np.asarray(x, np.float32).astype(ml_dtypes.bfloat16).astype(np.float64), axis, -1)
    blocks = v.reshape(v.shape[:-1] + (-1, 32))
    amax = np.abs(blocks).max(-1, keepdims=True)
    byte = np.maximum(np.where(amax > 0, np.frexp(amax)[1] - 1 + 127, 0) - down, 1)
    scale = np.exp2(byte - 127.0)
    codes = (blocks / scale).astype(np.float32).astype(dtype).astype(np.float64)
    return np.moveaxis((codes * scale).reshape(v.shape), -1, axis)


WIDE = False


def mx_kscale(k):
    if not WIDE:
        return np.ones(k)
    levels = np.array([10, -10, 5, -5, 0])
    if k % 512:
        return np.exp2(np.random.permutation(np.resize(levels, k // 32))).repeat(32)
    a = np.empty((k // 512, 16))
    for p in range(k // 512):
        a[p, :8] = np.random.permutation(np.resize(levels, 8))
        for g in range(8):
            far = levels[np.abs(levels - a[p, g]) >= 10]
            a[p, g + 8] = far[np.random.randint(len(far))]
    return np.exp2(a.ravel()).repeat(32)


def f64(x):
    return np.asarray(x).astype(np.float64)


def striped(idx):
    return np.tile(idx.reshape(-1, 16).T, (8, 1)).astype(np.uint16)


def unstriped(offs):
    return offs[:16].T.reshape(-1).astype(np.int64)


E2M1 = np.array([0.0, 0.5, 1.0, 1.5, 2.0, 3.0, 4.0, 6.0, -0.0, -0.5, -1.0, -1.5, -2.0, -3.0, -4.0, -6.0])


def pack_weight(w, fmt):
    k, n = w.shape
    w = f64(np.asarray(w, np.float32).astype(ml_dtypes.bfloat16)).reshape(k // 32, 32, n)
    amax = np.abs(w).max(1)
    if fmt == "e4m3":
        byte = np.frexp(amax)[1] - 1 + 127 - 7
    else:
        mant, ex = np.frexp(amax / 6.0)
        byte = np.where(mant > 0.5, ex, ex - 1) + 127
    byte = np.clip(np.where(amax > 0, byte, 1), 1, 254)
    scaled = (w * np.exp2(127.0 - byte)[:, None, :]).reshape(k, n).astype(np.float32)
    by_word = np.ascontiguousarray(scaled.reshape(k // 512, 128, 4, n).transpose(0, 1, 3, 2))
    if fmt == "e4m3":
        words = by_word.astype(ml_dtypes.float8_e4m3fn).view(np.uint8)
    else:
        c = by_word.astype(ml_dtypes.float4_e2m1fn).view(np.uint8) & 0xF
        words = (c[..., 0::2] | (c[..., 1::2] << 4)).reshape(k // 512, 128, 2 * n)
    return np.ascontiguousarray(words), np.ascontiguousarray(byte.astype(np.uint8).reshape(k // 512, 16, n))


def unpack_weight(words, scales, fmt):
    g, _, n = scales.shape
    words = np.ascontiguousarray(words).reshape(g, 128, n, -1)
    if fmt == "e4m3":
        vals = words.view(ml_dtypes.float8_e4m3fn).astype(np.float64)
    else:
        nib = np.empty((g, 128, n, 4), np.uint8)
        nib[..., 0::2] = words & 0xF
        nib[..., 1::2] = words >> 4
        vals = E2M1[nib]
    vals = vals * np.repeat(np.exp2(scales.astype(np.float64) - 127.0), 8, axis=1)[..., None]
    return vals.transpose(0, 1, 3, 2).reshape(g * 512, n)


def gelu(v):
    return 0.5 * v * (1.0 + np.tanh(np.sqrt(2.0 / np.pi) * (v + 0.044715 * v**3)))


def striped8(idx):
    return np.concatenate([v.reshape(-1, 16).T for v in idx]).astype(np.uint16)


def unstriped8(offs):
    return np.stack([offs[16 * g:16 * g + 16].T.reshape(-1) for g in range(8)]).astype(np.int64)


def runs(v, idx8):
    k = np.arange(v.shape[0])
    return v[k[:, None], idx8[k % 512 // 64]]


K, T, S, H, P, N = 1024, 2048, 1024, 1024, 512, 512

def setup_inputs():
    n = np.random.standard_normal
    s = mx_kscale(K)[:, None]
    u = mx_kscale(H)[:, None]
    tab_words, tab_scales = pack_weight(n((K, T)) * s, "e4m3")
    w2_words, w2_scales = pack_weight(n((H, N)) / np.sqrt(H) / u, "e2m1")
    arms = np.stack([np.random.permutation(S)[:P] for _ in range(8)])
    signs = np.random.choice([-1.0, 1.0], H)
    return {
        "tab_words": tab_words, "tab_scales": tab_scales,
        "offs": striped(np.random.permutation(T)[:S]),
        "offs2": striped8(arms),
        "w1": (n((K, H)) / np.sqrt(K) / s).astype(np.float32),
        "level": np.random.uniform(0.4, 1.0, H).astype(np.float32),
        "firn": (0.45 * n((H, S))).astype(np.float32),
        "sharp": np.repeat(np.random.uniform(1, 3, H // 64), 64).astype(np.float32),
        "share": np.repeat(np.random.uniform(0.1, 0.5, H // 64), 64).astype(np.float32),
        "gain": (signs * np.random.uniform(0.8, 2.4, H) * u[:, 0]).astype(np.float32),
        "w2_words": w2_words, "w2_scales": w2_scales,
        "mark": (0.4 * n(N)).astype(np.float32),
    }

def reference(tab_words, tab_scales, offs, offs2, w1, level, firn, sharp, share, gain, w2_words, w2_scales, mark):
    v = unpack_weight(tab_words, tab_scales, "e4m3")[:, unstriped(offs)]
    h = (mxq(f64(w1), 0, "e4m3").T @ v) * f64(level)[:, None] + f64(firn)
    top = h.max(axis=1)
    hp = runs(h, unstriped8(offs2))
    gate = 1.0 / (1.0 + np.exp(-f64(sharp)[:, None] * (hp - f64(share)[:, None] * top[:, None])))
    e = hp * gate * f64(gain)[:, None]
    w2 = unpack_weight(w2_words, w2_scales, "e2m1")
    y = w2.T @ mxq(e, 0, "e4m3")
    return np.maximum(y, f64(mark)[:, None])

@@ -1,0 +1,325 @@
+from contextlib import ExitStack
+
+import concourse.mybir as mybir
+
+K, T, S, H, M, N = 1024, 2048, 1024, 1024, 512, 512
+FLOPS = 2 * K * H * S + 2 * H * N * M
+
+F32 = mybir.dt.float32
+BF16 = mybir.dt.bfloat16
+I32 = mybir.dt.int32
+U32 = mybir.dt.uint32
+U16 = mybir.dt.uint16
+U8 = mybir.dt.uint8
+FP8X4 = mybir.dt.float8_e4m3fn_x4
+FP4X4 = mybir.dt.float4_e2m1fn_x4
+ALU = mybir.AluOpType
+ACT = mybir.ActivationFunctionType
+AXIS = mybir.AxisListType
+
+P = 128
+PACK = 4
+PASS = P * PACK
+BANK = 512
+HALF = M // 2
+
+
+def tile_list_bed_echo_marker_kernel(
+    tc, tab_words, tab_scales, offs, offs2, w1, level, firn, sharp, share, gain, w2_words, w2_scales, mark, out
+):
+    nc = tc.nc
+    n_tiles = H // P
+
+    with ExitStack() as ctx:
+        keep = ctx.enter_context(tc.tile_pool(name="keep", bufs=1))
+        ring = ctx.enter_context(tc.tile_pool(name="ring", bufs=4))
+        acc_pool = ctx.enter_context(tc.psum_pool(name="acc", bufs=4))
+        y_pool = ctx.enter_context(tc.psum_pool(name="y", bufs=1))
+
+        def held(shape, dtype, name, tag=None):
+            return keep.tile(shape, dtype, name=name, tag=tag or name, align_bytes=64)
+
+        trace_list = held([P, S // 16], U16, "trace_list")
+        arm_lists = held([P, M // 16], U16, "arm_lists")
+        tab_w = [held([P, T], I32, "tab_w%d" % a) for a in range(2)]
+        tab_s = held([P, T], U8, "tab_s")
+        w1_raw = {(a, b): held([P, PACK, PASS], F32, "w1_raw%d%d" % (a, b)) for a in range(2) for b in range(2)}
+        firn_t = [held([P, S], F32, "firn%d" % t) for t in range(n_tiles)]
+        level_t = held([P, 2, PACK], F32, "level_t")
+        sharp_t = held([P, 2, PACK], F32, "sharp_t")
+        share_t = held([P, 2, PACK], F32, "share_t")
+        gain_t = held([P, 2, PACK], F32, "gain_t")
+        mark_t = held([P, N // P], F32, "mark_t")
+        w2_w = held([P, 2, 2 * N], U8, "w2_w")
+        w2_s = held([P, 2, N], U8, "w2_s")
+
+        def load_w1(a, b):
+            rows = w1[PASS * a : PASS * (a + 1), PASS * b : PASS * (b + 1)]
+            nc.sync.dma_start(out=w1_raw[a, b][:], in_=rows.rearrange("(p j) c -> p j c", j=PACK))
+
+        def load_firn(t):
+            b, i = divmod(t, PACK)
+            rows = firn[PASS * b : PASS * (b + 1), :].rearrange("(p i) j -> p i j", i=PACK)
+            nc.sync.dma_start(out=firn_t[t][:], in_=rows[:, i, :])
+
+        def load_words(a):
+            nc.sync.dma_start(out=tab_w[a][:], in_=tab_words[a].rearrange("p t i -> p (t i)").bitcast(I32))
+
+        def load_rows(tile, vec):
+            nc.sync.dma_start(out=tile[:], in_=vec.rearrange("(b p i) -> p b i", b=2, i=PACK))
+
+        nc.gpsimd.memset(tab_s[:].bitcast(I32), 0)
+        nc.gpsimd.memset(w2_s[:].rearrange("p a n -> p (a n)").bitcast(I32), 0)
+        nc.sync.dma_start(out=trace_list[:], in_=offs)
+        load_w1(0, 0)
+        for q in range(4):
+            nc.sync.dma_start(
+                out=tab_s[32 * q : 32 * q + 8, :].bitcast(I32), in_=tab_scales[:, 4 * q : 4 * q + 4, :].bitcast(I32)
+            )
+        load_words(0)
+        load_words(1)
+        load_w1(1, 0)
+        load_rows(level_t, level)
+        load_firn(0)
+        nc.sync.dma_start(out=arm_lists[:], in_=offs2)
+        load_rows(sharp_t, sharp)
+        load_rows(share_t, share)
+        load_firn(1)
+        load_rows(gain_t, gain)
+        load_w1(0, 1)
+        load_firn(2)
+        load_w1(1, 1)
+        for t in range(3, n_tiles):
+            load_firn(t)
+        nc.sync.dma_start(out=w2_w[:].bitcast(I32), in_=w2_words.rearrange("a p n -> p a n").bitcast(I32))
+        for q in range(4):
+            nc.sync.dma_start(
+                out=w2_s[32 * q : 32 * q + 4, :, :].bitcast(I32),
+                in_=w2_scales[:, 4 * q : 4 * q + 4, :].rearrange("a r n -> r a n").bitcast(I32),
+            )
+        with nc.allow_non_contiguous_dma(reason="one value of mark for each partition"):
+            nc.sync.dma_start(out=mark_t[:], in_=mark.rearrange("(c p) -> p c", p=P))
+
+        v_s = held([P, S], U8, "v_s")
+        v_w = {(a, u): held([P, BANK], U32, "v_w%d%d" % (a, u)) for a in range(2) for u in range(2)}
+
+        def gather_words(a):
+            for u in range(2):
+                cols = trace_list[:, 32 * u : 32 * (u + 1)]
+                nc.vector.tensor_copy(out=v_w[a, u][:], in_=tab_w[a][:].bitcast(U32).indirect(cols))
+
+        w1_bf = {}
+        w1_w = {}
+        w1_s = {}
+
+        def round_w1(a, b, pair, engine):
+            key = (a, b, pair)
+            w1_bf[key] = held([P, 2, P, PACK], BF16, "w1_bf%d%d%d" % key)
+            src = w1_raw[a, b][:].rearrange("p j (m t) -> p m j t", t=PACK)[:, :, :, 2 * pair : 2 * pair + 2]
+            dst = w1_bf[key][:].rearrange("p t m j -> p m j t")
+            if engine == "scalar":
+                nc.scalar.copy(out=dst, in_=src)
+            elif engine == "gpsimd":
+                nc.gpsimd.tensor_scalar(
+                    out=dst.rearrange("p m j t -> p m t j"),
+                    in0=src.rearrange("p m j t -> p m t j"),
+                    scalar1=1.0,
+                    scalar2=1.0,
+                    op0=ALU.mult,
+                    op1=ALU.mult,
+                )
+            else:
+                nc.vector.tensor_copy(out=dst, in_=src)
+
+        def quantize_w1(a, b, pair):
+            key = (a, b, pair)
+            w1_w[key] = held([P, 2 * P], U32, "w1_w%d%d%d" % key)
+            w1_s[key] = held([P, 2 * P], U8, "w1_s%d%d%d" % key)
+            nc.vector.quantize_mx(
+                out=w1_w[key][:].bitcast(FP8X4),
+                scales=w1_s[key][:],
+                in_=w1_bf[key][:].rearrange("p t m j -> p (t m j)"),
+            )
+
+        nc.vector.tensor_copy(out=v_s[:], in_=tab_s[:].indirect(trace_list[:]))
+        round_w1(0, 0, 0, "scalar")
+        round_w1(0, 0, 1, "scalar")
+        gather_words(0)
+        quantize_w1(0, 0, 0)
+        gather_words(1)
+        round_w1(1, 0, 0, "scalar")
+        round_w1(1, 0, 1, "scalar")
+        quantize_w1(0, 0, 1)
+        quantize_w1(1, 0, 0)
+
+        slope = held([P, 2, PACK], F32, "slope")
+        nc.vector.scalar_tensor_tensor(
+            out=slope[:].rearrange("p b i -> p (b i)"),
+            in0=sharp_t[:].rearrange("p b i -> p (b i)"),
+            scalar=-1.0,
+            in1=share_t[:].rearrange("p b i -> p (b i)"),
+            op0=ALU.mult,
+            op1=ALU.mult,
+        )
+
+        h = [held([P, S], F32, "h%d" % t) for t in range(n_tiles)]
+        top = held([P, n_tiles], F32, "top")
+        shift = held([P, n_tiles], F32, "shift")
+        e_rows = [held([P, PACK, M], BF16, "e_rows%d" % b) for b in range(2)]
+        picked = {}
+        gate = {}
+
+        def column(tile, t):
+            b, i = divmod(t, PACK)
+            return tile[:, b, i : i + 1]
+
+        def make_shift(t):
+            nc.vector.tensor_scalar(
+                out=shift[:, t : t + 1], in0=top[:, t : t + 1], scalar1=column(slope, t), scalar2=None, op0=ALU.mult
+            )
+
+        def make_h(t):
+            b, i = divmod(t, PACK)
+            pair, within = divmod(i, 2)
+            cols = slice(P * within, P * (within + 1))
+            for u in range(2):
+                acc = acc_pool.tile([P, BANK], F32, name="acc")
+                for a in range(2):
+                    nc.tensor.matmul_mx(
+                        out=acc[:],
+                        lhsT=w1_w[a, b, pair][:, cols].bitcast(FP8X4),
+                        lhsT_scale=w1_s[a, b, pair][:, cols],
+                        rhs=v_w[a, u][:].bitcast(FP8X4),
+                        rhs_scale=v_s[4 * a : P, BANK * u : BANK * (u + 1)],
+                        start=(a == 0),
+                        stop=(a == 1),
+                    )
+                nc.vector.scalar_tensor_tensor(
+                    out=h[t][:, BANK * u : BANK * (u + 1)],
+                    in0=acc[:],
+                    scalar=column(level_t, t),
+                    in1=firn_t[t][:, BANK * u : BANK * (u + 1)],
+                    op0=ALU.mult,
+                    op1=ALU.add,
+                )
+
+        def look(t, spans):
+            picked[t] = ring.tile([P, M], F32, name="picked")
+            gate[t] = ring.tile([P, M], F32, name="gate")
+            nc.vector.tensor_reduce(out=top[:, t : t + 1], in_=h[t][:], axis=AXIS.X, op=ALU.max)
+            nc.scalar.activation(out=picked[t][:], in_=h[t][:].indirect(arm_lists[:]), func=ACT.Copy)
+            make_shift(t)
+            for lo, hi in spans:
+                nc.scalar.activation(
+                    out=gate[t][:, lo:hi],
+                    in_=h[t][:].indirect(arm_lists[:, lo // 16 : hi // 16]),
+                    func=ACT.Sigmoid,
+                    bias=shift[:, t : t + 1],
+                    scale=column(sharp_t, t),
+                )
+
+        def make_e(t, lo, hi):
+            b, i = divmod(t, PACK)
+            nc.vector.scalar_tensor_tensor(
+                out=e_rows[b][:, i, lo:hi],
+                in0=picked[t][:, lo:hi],
+                scalar=column(gain_t, t),
+                in1=gate[t][:, lo:hi],
+                op0=ALU.mult,
+                op1=ALU.mult,
+            )
+
+        def make_e_gpsimd(t):
+            b, i = divmod(t, PACK)
+            scaled = ring.tile([P, M], F32, name="scaled")
+            nc.gpsimd.tensor_scalar(
+                out=scaled[:], in0=picked[t][:], scalar1=column(gain_t, t), scalar2=1.0, op0=ALU.mult, op1=ALU.mult
+            )
+            nc.gpsimd.tensor_tensor(out=e_rows[b][:, i, :], in0=scaled[:], in1=gate[t][:], op=ALU.mult)
+
+        e_bf = {}
+        e_w = {}
+        e_s = {}
+
+        def weave_e(b, lo, hi, tag=None):
+            e_bf[b, lo] = held([P, hi - lo, PACK], BF16, "e_bf%d%d" % (b, lo), tag)
+            nc.vector.tensor_copy(
+                out=e_bf[b, lo][:].rearrange("p (c q) i -> p c i q", q=4),
+                in_=e_rows[b][:, :, lo:hi].rearrange("p i (c q) -> p c i q", q=4),
+            )
+
+        def quantize_e(b, lo, hi):
+            words = held([P, hi - lo], U32, "e_w%d%d" % (b, lo))
+            planes = held([P, hi - lo], U8, "e_s%d%d" % (b, lo))
+            nc.vector.quantize_mx(
+                out=words[:].bitcast(FP8X4), scales=planes[:], in_=e_bf[b, lo][:].rearrange("p m i -> p (m i)")
+            )
+            for start in range(lo, hi, HALF):
+                e_w[b, start // HALF] = words[:, start - lo : start - lo + HALF]
+                e_s[b, start // HALF] = planes[:, start - lo : start - lo + HALF]
+
+        y = {(u, g): y_pool.tile([P, 2, HALF], F32, name="y%d%d" % (u, g)) for u in range(2) for g in range(2)}
+
+        def score(b, u):
+            for c in range(N // P):
+                g, within = divmod(c, 2)
+                nc.tensor.matmul_mx(
+                    out=y[u, g][:, within, :],
+                    lhsT=w2_w[:, b, 2 * P * c : 2 * P * (c + 1)].bitcast(FP4X4),
+                    lhsT_scale=w2_s[:, b, P * c : P * (c + 1)],
+                    rhs=e_w[b, u].bitcast(FP8X4),
+                    rhs_scale=e_s[b, u],
+                    start=(b == 0 and within == 0),
+                    stop=(b == 1 and within == 1),
+                )
+
+        def finish(u):
+            for g in range(2):
+                res = held([P, 2, HALF], F32, "res%d%d" % (u, g))
+                for within in range(2):
+                    c = 2 * g + within
+                    nc.vector.tensor_scalar(
+                        out=res[:, within, :],
+                        in0=y[u, g][:, within, :],
+                        scalar1=mark_t[:, c : c + 1],
+                        scalar2=None,
+                        op0=ALU.max,
+                    )
+                rows = out[2 * P * g : 2 * P * (g + 1), HALF * u : HALF * (u + 1)]
+                nc.sync.dma_start(out=rows.rearrange("(c p) m -> p c m", p=P), in_=res[:])
+
+        whole = [(0, M)]
+        halves = [(0, HALF), (HALF, M)]
+        last = n_tiles - 1
+        for t in range(n_tiles):
+            make_h(t)
+            if t == 0:
+                quantize_w1(1, 0, 1)
+            look(t, halves if t == last else whole)
+            if t == 1:
+                round_w1(0, 1, 0, "vector")
+                round_w1(0, 1, 1, "gpsimd")
+            if t == 2:
+                round_w1(1, 1, 0, "vector")
+                round_w1(1, 1, 1, "gpsimd")
+                quantize_w1(0, 1, 0)
+                quantize_w1(1, 1, 0)
+            if t == 4:
+                quantize_w1(0, 1, 1)
+                quantize_w1(1, 1, 1)
+            if t < last:
+                make_e_gpsimd(t)
+        weave_e(0, 0, M, "firn%d" % last)
+        quantize_e(0, 0, M)
+        score(0, 0)
+        score(0, 1)
+        make_e(last, 0, HALF)
+        weave_e(1, 0, HALF)
+        make_e(last, HALF, M)
+        quantize_e(1, 0, HALF)
+        weave_e(1, HALF, M)
+        score(1, 0)
+        quantize_e(1, HALF, M)
+        finish(0)
+        score(1, 1)
+        finish(1)

@@ -29,10 +29,10 @@ def tile_list_bed_echo_marker_kernel(
 ):
     nc = tc.nc
     n_tiles = H // P
+    last = n_tiles - 1
 
     with ExitStack() as ctx:
         keep = ctx.enter_context(tc.tile_pool(name="keep", bufs=1))
-        ring = ctx.enter_context(tc.tile_pool(name="ring", bufs=4))
         acc_pool = ctx.enter_context(tc.psum_pool(name="acc", bufs=4))
         y_pool = ctx.enter_context(tc.psum_pool(name="y", bufs=1))
 
@@ -43,7 +43,6 @@ def tile_list_bed_echo_marker_kernel(
         arm_lists = held([P, M // 16], U16, "arm_lists")
         tab_w = [held([P, T], I32, "tab_w%d" % a) for a in range(2)]
         tab_s = held([P, T], U8, "tab_s")
-        w1_raw = {(a, b): held([P, PACK, PASS], F32, "w1_raw%d%d" % (a, b)) for a in range(2) for b in range(2)}
         firn_t = [held([P, S], F32, "firn%d" % t) for t in range(n_tiles)]
         level_t = held([P, 2, PACK], F32, "level_t")
         sharp_t = held([P, 2, PACK], F32, "sharp_t")
@@ -52,10 +51,13 @@ def tile_list_bed_echo_marker_kernel(
         mark_t = held([P, N // P], F32, "mark_t")
         w2_w = held([P, 2, 2 * N], U8, "w2_w")
         w2_s = held([P, 2, N], U8, "w2_s")
+        w1_raw = {}
 
-        def load_w1(a, b):
-            rows = w1[PASS * a : PASS * (a + 1), PASS * b : PASS * (b + 1)]
-            nc.sync.dma_start(out=w1_raw[a, b][:], in_=rows.rearrange("(p j) c -> p j c", j=PACK))
+        def load_w1(a, b, lo, hi):
+            raw = held([P, PACK, PACK * (hi - lo)], F32, "w1_raw%d%d_%d" % (a, b, lo))
+            rows = w1[PASS * a : PASS * (a + 1), PASS * b + PACK * lo : PASS * b + PACK * hi]
+            nc.sync.dma_start(out=raw[:], in_=rows.rearrange("(p j) c -> p j c", j=PACK))
+            w1_raw.setdefault((a, b), []).append((lo, hi, raw))
 
         def load_firn(t):
             b, i = divmod(t, PACK)
@@ -71,25 +73,25 @@ def tile_list_bed_echo_marker_kernel(
         nc.gpsimd.memset(tab_s[:].bitcast(I32), 0)
         nc.gpsimd.memset(w2_s[:].rearrange("p a n -> p (a n)").bitcast(I32), 0)
         nc.sync.dma_start(out=trace_list[:], in_=offs)
-        load_w1(0, 0)
+        load_w1(0, 0, 0, P)
         for q in range(4):
             nc.sync.dma_start(
                 out=tab_s[32 * q : 32 * q + 8, :].bitcast(I32), in_=tab_scales[:, 4 * q : 4 * q + 4, :].bitcast(I32)
             )
         load_words(0)
         load_words(1)
-        load_w1(1, 0)
+        load_w1(1, 0, 0, P // 2)
+        load_w1(1, 0, P // 2, P)
         load_rows(level_t, level)
         load_firn(0)
         nc.sync.dma_start(out=arm_lists[:], in_=offs2)
         load_rows(sharp_t, sharp)
         load_rows(share_t, share)
+        load_w1(0, 1, 0, P)
+        load_w1(1, 1, 0, P)
         load_firn(1)
         load_rows(gain_t, gain)
-        load_w1(0, 1)
-        load_firn(2)
-        load_w1(1, 1)
-        for t in range(3, n_tiles):
+        for t in range(2, n_tiles):
             load_firn(t)
         nc.sync.dma_start(out=w2_w[:].bitcast(I32), in_=w2_words.rearrange("a p n -> p a n").bitcast(I32))
         for q in range(4):
@@ -112,71 +114,71 @@ def tile_list_bed_echo_marker_kernel(
         w1_w = {}
         w1_s = {}
 
-        def round_w1(a, b, pair, engine):
-            key = (a, b, pair)
-            w1_bf[key] = held([P, 2, P, PACK], BF16, "w1_bf%d%d%d" % key)
-            src = w1_raw[a, b][:].rearrange("p j (m t) -> p m j t", t=PACK)[:, :, :, 2 * pair : 2 * pair + 2]
-            dst = w1_bf[key][:].rearrange("p t m j -> p m j t")
-            if engine == "scalar":
-                nc.scalar.copy(out=dst, in_=src)
-            elif engine == "gpsimd":
-                nc.gpsimd.tensor_scalar(
-                    out=dst.rearrange("p m j t -> p m t j"),
-                    in0=src.rearrange("p m j t -> p m t j"),
-                    scalar1=1.0,
-                    scalar2=1.0,
-                    op0=ALU.mult,
-                    op1=ALU.mult,
-                )
-            else:
-                nc.vector.tensor_copy(out=dst, in_=src)
+        def round_w1(a, b, pair, engines, tag=None):
+            if a == 0:
+                w1_bf[b, pair] = held([P, 2, 2, P, PACK], BF16, "w1_bf%d%d" % (b, pair), tag)
+            for (lo, hi, raw), engine in zip(w1_raw[a, b], engines):
+                src = raw[:].rearrange("p j (m t) -> p m j t", t=PACK)[:, :, :, 2 * pair : 2 * pair + 2]
+                dst = w1_bf[b, pair][:, a, :, lo:hi, :].rearrange("p t m j -> p m j t")
+                if engine == "scalar":
+                    nc.scalar.copy(out=dst, in_=src)
+                elif engine == "gpsimd":
+                    nc.gpsimd.tensor_scalar(
+                        out=dst.rearrange("p m j t -> p m t j"),
+                        in0=src.rearrange("p m j t -> p m t j"),
+                        scalar1=1.0,
+                        scalar2=1.0,
+                        op0=ALU.mult,
+                        op1=ALU.mult,
+                    )
+                else:
+                    nc.vector.tensor_copy(out=dst, in_=src)
 
-        def quantize_w1(a, b, pair):
-            key = (a, b, pair)
-            w1_w[key] = held([P, 2 * P], U32, "w1_w%d%d%d" % key)
-            w1_s[key] = held([P, 2 * P], U8, "w1_s%d%d%d" % key)
+        def quantize_w1(passes, b, pair, tag=None):
+            first, count = passes[0], len(passes)
+            words = held([P, 2 * P * count], U32, "w1_w%d%d%d" % (first, b, pair), tag)
+            planes = held([P, 2 * P * count], U8, "w1_s%d%d%d" % (first, b, pair))
             nc.vector.quantize_mx(
-                out=w1_w[key][:].bitcast(FP8X4),
-                scales=w1_s[key][:],
-                in_=w1_bf[key][:].rearrange("p t m j -> p (t m j)"),
+                out=words[:].bitcast(FP8X4),
+                scales=planes[:],
+                in_=w1_bf[b, pair][:, first : first + count, :, :, :].rearrange("p a t m j -> p (a t m j)"),
             )
+            for a in passes:
+                w1_w[a, b, pair] = words[:, 2 * P * (a - first) : 2 * P * (a - first + 1)]
+                w1_s[a, b, pair] = planes[:, 2 * P * (a - first) : 2 * P * (a - first + 1)]
 
         nc.vector.tensor_copy(out=v_s[:], in_=tab_s[:].indirect(trace_list[:]))
-        round_w1(0, 0, 0, "scalar")
-        round_w1(0, 0, 1, "scalar")
+        round_w1(0, 0, 0, ["scalar"])
         gather_words(0)
-        quantize_w1(0, 0, 0)
+        quantize_w1([0], 0, 0)
+        round_w1(0, 0, 1, ["scalar"])
         gather_words(1)
-        round_w1(1, 0, 0, "scalar")
-        round_w1(1, 0, 1, "scalar")
-        quantize_w1(0, 0, 1)
-        quantize_w1(1, 0, 0)
+        round_w1(1, 0, 0, ["scalar", "vector"])
+        quantize_w1([1], 0, 0)
+        round_w1(1, 0, 1, ["scalar", "scalar"])
 
-        slope = held([P, 2, PACK], F32, "slope")
-        nc.vector.scalar_tensor_tensor(
-            out=slope[:].rearrange("p b i -> p (b i)"),
-            in0=sharp_t[:].rearrange("p b i -> p (b i)"),
-            scalar=-1.0,
-            in1=share_t[:].rearrange("p b i -> p (b i)"),
-            op0=ALU.mult,
-            op1=ALU.mult,
-        )
+        top_slope = []
+        for lo, hi in [(0, last), (last, n_tiles)]:
+            pairs = held([P, hi - lo, 2], F32, "top_slope%d" % lo)
+            nc.vector.scalar_tensor_tensor(
+                out=pairs[:, :, 1],
+                in0=sharp_t[:].rearrange("p b i -> p (b i)")[:, lo:hi],
+                scalar=-1.0,
+                in1=share_t[:].rearrange("p b i -> p (b i)")[:, lo:hi],
+                op0=ALU.mult,
+                op1=ALU.mult,
+            )
+            top_slope.extend(pairs[:, t, :] for t in range(hi - lo))
 
         h = [held([P, S], F32, "h%d" % t) for t in range(n_tiles)]
-        top = held([P, n_tiles], F32, "top")
         shift = held([P, n_tiles], F32, "shift")
-        e_rows = [held([P, PACK, M], BF16, "e_rows%d" % b) for b in range(2)]
-        picked = {}
-        gate = {}
+        picked = [held([P, M], F32, "picked%d" % t) for t in range(n_tiles)]
+        gate = [held([P, M], F32, "gate%d" % t) for t in range(n_tiles)]
+        e_rows = {}
 
         def column(tile, t):
             b, i = divmod(t, PACK)
             return tile[:, b, i : i + 1]
-
-        def make_shift(t):
-            nc.vector.tensor_scalar(
-                out=shift[:, t : t + 1], in0=top[:, t : t + 1], scalar1=column(slope, t), scalar2=None, op0=ALU.mult
-            )
 
         def make_h(t):
             b, i = divmod(t, PACK)
@@ -204,11 +206,9 @@ def tile_list_bed_echo_marker_kernel(
                 )
 
         def look(t, spans):
-            picked[t] = ring.tile([P, M], F32, name="picked")
-            gate[t] = ring.tile([P, M], F32, name="gate")
-            nc.vector.tensor_reduce(out=top[:, t : t + 1], in_=h[t][:], axis=AXIS.X, op=ALU.max)
+            nc.vector.tensor_reduce(out=top_slope[t][:, 0:1], in_=h[t][:], axis=AXIS.X, op=ALU.max)
             nc.scalar.activation(out=picked[t][:], in_=h[t][:].indirect(arm_lists[:]), func=ACT.Copy)
-            make_shift(t)
+            nc.vector.tensor_reduce(out=shift[:, t : t + 1], in_=top_slope[t], axis=AXIS.X, op=ALU.mult)
             for lo, hi in spans:
                 nc.scalar.activation(
                     out=gate[t][:, lo:hi],
@@ -229,9 +229,9 @@ def tile_list_bed_echo_marker_kernel(
                 op1=ALU.mult,
             )
 
-        def make_e_gpsimd(t):
+        def make_e_gpsimd(t, tag):
             b, i = divmod(t, PACK)
-            scaled = ring.tile([P, M], F32, name="scaled")
+            scaled = held([P, M], F32, "scaled%d" % t, tag)
             nc.gpsimd.tensor_scalar(
                 out=scaled[:], in0=picked[t][:], scalar1=column(gain_t, t), scalar2=1.0, op0=ALU.mult, op1=ALU.mult
             )
@@ -241,15 +241,27 @@ def tile_list_bed_echo_marker_kernel(
         e_w = {}
         e_s = {}
 
-        def weave_e(b, lo, hi, tag=None):
+        def weave_e(b, lo, hi, engine, tag=None):
             e_bf[b, lo] = held([P, hi - lo, PACK], BF16, "e_bf%d%d" % (b, lo), tag)
-            nc.vector.tensor_copy(
-                out=e_bf[b, lo][:].rearrange("p (c q) i -> p c i q", q=4),
-                in_=e_rows[b][:, :, lo:hi].rearrange("p i (c q) -> p c i q", q=4),
-            )
+            if engine == "gpsimd":
+                nc.gpsimd.tensor_scalar(
+                    out=e_bf[b, lo][:],
+                    in0=e_rows[b][:, :, lo:hi].rearrange("p i m -> p m i"),
+                    scalar1=1.0,
+                    scalar2=1.0,
+                    op0=ALU.mult,
+                    op1=ALU.mult,
+                )
+            else:
+                dst = e_bf[b, lo][:].rearrange("p (c q) i -> p c i q", q=4)
+                src = e_rows[b][:, :, lo:hi].rearrange("p i (c q) -> p c i q", q=4)
+                if engine == "scalar":
+                    nc.scalar.copy(out=dst, in_=src)
+                else:
+                    nc.vector.tensor_copy(out=dst, in_=src)
 
-        def quantize_e(b, lo, hi):
-            words = held([P, hi - lo], U32, "e_w%d%d" % (b, lo))
+        def quantize_e(b, lo, hi, tag=None):
+            words = held([P, hi - lo], U32, "e_w%d%d" % (b, lo), tag)
             planes = held([P, hi - lo], U8, "e_s%d%d" % (b, lo))
             nc.vector.quantize_mx(
                 out=words[:].bitcast(FP8X4), scales=planes[:], in_=e_bf[b, lo][:].rearrange("p m i -> p (m i)")
@@ -273,11 +285,23 @@ def tile_list_bed_echo_marker_kernel(
                     stop=(b == 1 and within == 1),
                 )
 
-        def finish(u):
-            for g in range(2):
-                res = held([P, 2, HALF], F32, "res%d%d" % (u, g))
-                for within in range(2):
-                    c = 2 * g + within
+        def finish(u, g, engine):
+            res = held([P, 2, HALF], F32, "res%d%d" % (u, g))
+            if engine == "gpsimd":
+                sums = held([P, 2, HALF], F32, "sums%d%d" % (u, g), "h%d" % (2 * u + g))
+                nc.scalar.copy(out=sums[:], in_=y[u, g][:])
+            for within in range(2):
+                c = 2 * g + within
+                if engine == "gpsimd":
+                    nc.gpsimd.tensor_scalar(
+                        out=res[:, within, :],
+                        in0=sums[:, within, :],
+                        scalar1=3.0e38,
+                        scalar2=mark_t[:, c : c + 1],
+                        op0=ALU.min,
+                        op1=ALU.max,
+                    )
+                else:
                     nc.vector.tensor_scalar(
                         out=res[:, within, :],
                         in0=y[u, g][:, within, :],
@@ -285,41 +309,44 @@ def tile_list_bed_echo_marker_kernel(
                         scalar2=None,
                         op0=ALU.max,
                     )
-                rows = out[2 * P * g : 2 * P * (g + 1), HALF * u : HALF * (u + 1)]
-                nc.sync.dma_start(out=rows.rearrange("(c p) m -> p c m", p=P), in_=res[:])
+            rows = out[2 * P * g : 2 * P * (g + 1), HALF * u : HALF * (u + 1)]
+            nc.sync.dma_start(out=rows.rearrange("(c p) m -> p c m", p=P), in_=res[:])
 
         whole = [(0, M)]
         halves = [(0, HALF), (HALF, M)]
-        last = n_tiles - 1
         for t in range(n_tiles):
             make_h(t)
-            if t == 0:
-                quantize_w1(1, 0, 1)
             look(t, halves if t == last else whole)
-            if t == 1:
-                round_w1(0, 1, 0, "vector")
-                round_w1(0, 1, 1, "gpsimd")
-            if t == 2:
-                round_w1(1, 1, 0, "vector")
-                round_w1(1, 1, 1, "gpsimd")
-                quantize_w1(0, 1, 0)
-                quantize_w1(1, 1, 0)
-            if t == 4:
-                quantize_w1(0, 1, 1)
-                quantize_w1(1, 1, 1)
-            if t < last:
-                make_e_gpsimd(t)
-        weave_e(0, 0, M, "firn%d" % last)
-        quantize_e(0, 0, M)
+            if t == 0:
+                quantize_w1([0, 1], 0, 1, "firn0")
+                round_w1(0, 1, 0, ["vector"])
+                round_w1(1, 1, 0, ["vector"])
+                quantize_w1([0, 1], 1, 0)
+                round_w1(0, 1, 1, ["scalar"])
+                round_w1(1, 1, 1, ["scalar"])
+            if t == 3:
+                quantize_w1([0, 1], 1, 1, "firn3")
+        e_rows[0] = held([P, PACK, M], BF16, "e_rows0")
+        for t in range(PACK):
+            make_e_gpsimd(t, "w1_bf10")
+        weave_e(0, 0, M, "gpsimd")
+        e_rows[1] = held([P, PACK, M], BF16, "e_rows1", "firn7")
+        for t in range(PACK, 4):
+            make_e_gpsimd(t, "w1_bf10")
+        quantize_e(0, 0, M, "top_slope7")
         score(0, 0)
         score(0, 1)
+        for t in range(4, last):
+            make_e(t, 0, M)
         make_e(last, 0, HALF)
-        weave_e(1, 0, HALF)
+        weave_e(1, 0, HALF, "vector")
         make_e(last, HALF, M)
         quantize_e(1, 0, HALF)
-        weave_e(1, HALF, M)
+        weave_e(1, HALF, M, "vector")
         score(1, 0)
         quantize_e(1, HALF, M)
-        finish(0)
+        finish(0, 0, "vector")
+        finish(0, 1, "vector")
         score(1, 1)
-        finish(1)
+        finish(1, 0, "vector")
+        finish(1, 1, "vector")

@@ -1,6 +1,7 @@
 from contextlib import ExitStack
 
 import concourse.mybir as mybir
+from concourse.masks import make_identity
 
 K, T, S, H, M, N = 1024, 2048, 1024, 1024, 512, 512
 FLOPS = 2 * K * H * S + 2 * H * N * M
@@ -44,11 +45,8 @@ def tile_list_bed_echo_marker_kernel(
         tab_w = [held([P, T], I32, "tab_w%d" % a) for a in range(2)]
         tab_s = held([P, T], U8, "tab_s")
         firn_t = [held([P, S], F32, "firn%d" % t) for t in range(n_tiles)]
-        level_t = held([P, 2, PACK], F32, "level_t")
-        sharp_t = held([P, 2, PACK], F32, "sharp_t")
-        share_t = held([P, 2, PACK], F32, "share_t")
-        gain_t = held([P, 2, PACK], F32, "gain_t")
-        mark_t = held([P, N // P], F32, "mark_t")
+        vec_rows = held([P, PASS], F32, "vec_rows")
+        identity = held([P, P], F32, "identity")
         w2_w = held([P, 2, 2 * N], U8, "w2_w")
         w2_s = held([P, 2, N], U8, "w2_s")
         w1_raw = {}
@@ -67,30 +65,28 @@ def tile_list_bed_echo_marker_kernel(
         def load_words(a):
             nc.sync.dma_start(out=tab_w[a][:], in_=tab_words[a].rearrange("p t i -> p (t i)").bitcast(I32))
 
-        def load_rows(tile, vec):
-            nc.sync.dma_start(out=tile[:], in_=vec.rearrange("(b p i) -> p b i", b=2, i=PACK))
-
         nc.gpsimd.memset(tab_s[:].bitcast(I32), 0)
+        nc.gpsimd.memset(vec_rows[:], 0.0)
+        make_identity(nc, identity[:])
         nc.gpsimd.memset(w2_s[:].rearrange("p a n -> p (a n)").bitcast(I32), 0)
         nc.sync.dma_start(out=trace_list[:], in_=offs)
-        load_w1(0, 0, 0, P)
+        nc.sync.dma_start(out=arm_lists[:], in_=offs2)
         for q in range(4):
             nc.sync.dma_start(
                 out=tab_s[32 * q : 32 * q + 8, :].bitcast(I32), in_=tab_scales[:, 4 * q : 4 * q + 4, :].bitcast(I32)
             )
         load_words(0)
         load_words(1)
+        for row, vec in enumerate([level, sharp, share, gain]):
+            nc.sync.dma_start(out=vec_rows[2 * row : 2 * row + 2, :], in_=vec.rearrange("(b c) -> b c", b=2))
+        nc.sync.dma_start(out=vec_rows[8:9, :], in_=mark.rearrange("(b c) -> b c", b=1))
+        load_w1(0, 0, 0, P)
         load_w1(1, 0, 0, P // 2)
         load_w1(1, 0, P // 2, P)
-        load_rows(level_t, level)
         load_firn(0)
-        nc.sync.dma_start(out=arm_lists[:], in_=offs2)
-        load_rows(sharp_t, sharp)
-        load_rows(share_t, share)
+        load_firn(1)
         load_w1(0, 1, 0, P)
         load_w1(1, 1, 0, P)
-        load_firn(1)
-        load_rows(gain_t, gain)
         for t in range(2, n_tiles):
             load_firn(t)
         nc.sync.dma_start(out=w2_w[:].bitcast(I32), in_=w2_words.rearrange("a p n -> p a n").bitcast(I32))
@@ -99,8 +95,18 @@ def tile_list_bed_echo_marker_kernel(
                 out=w2_s[32 * q : 32 * q + 4, :, :].bitcast(I32),
                 in_=w2_scales[:, 4 * q : 4 * q + 4, :].rearrange("a r n -> r a n").bitcast(I32),
             )
-        with nc.allow_non_contiguous_dma(reason="one value of mark for each partition"):
-            nc.sync.dma_start(out=mark_t[:], in_=mark.rearrange("(c p) -> p c", p=P))
+
+        by_row = held([P, 4, 2, PACK], F32, "by_row")
+        mark_t = held([P, N // P], F32, "mark_t")
+        turned = y_pool.tile([P, PACK, P], F32, name="turned", tag="y00")
+        turned_mark = y_pool.tile([P, N // P, P], F32, name="turned_mark", tag="y01")
+        for i in range(PACK):
+            nc.tensor.transpose(out=turned[:, i, :], in_=vec_rows[:, i:PASS:PACK], identity=identity[:])
+        for c in range(N // P):
+            nc.tensor.transpose(out=turned_mark[:, c, :], in_=vec_rows[:, P * c : P * (c + 1)], identity=identity[:])
+        nc.scalar.copy(out=by_row[:].rearrange("p v b i -> p (v b) i"), in_=turned[:, :, 0:8].rearrange("p i k -> p k i"))
+        nc.scalar.copy(out=mark_t[:], in_=turned_mark[:, :, 8])
+        level_t, sharp_t, share_t, gain_t = [by_row[:, v, :, :] for v in range(4)]
 
         v_s = held([P, S], U8, "v_s")
         v_w = {(a, u): held([P, BANK], U32, "v_w%d%d" % (a, u)) for a in range(2) for u in range(2)}
@@ -148,23 +154,25 @@ def tile_list_bed_echo_marker_kernel(
                 w1_s[a, b, pair] = planes[:, 2 * P * (a - first) : 2 * P * (a - first + 1)]
 
         nc.vector.tensor_copy(out=v_s[:], in_=tab_s[:].indirect(trace_list[:]))
-        round_w1(0, 0, 0, ["scalar"])
         gather_words(0)
-        quantize_w1([0], 0, 0)
-        round_w1(0, 0, 1, ["scalar"])
         gather_words(1)
-        round_w1(1, 0, 0, ["scalar", "vector"])
-        quantize_w1([1], 0, 0)
+        round_w1(0, 0, 0, ["vector"])
+        round_w1(0, 0, 1, ["scalar"])
+        quantize_w1([0], 0, 0)
+        quantize_w1([0], 0, 1)
+        round_w1(1, 0, 0, ["vector", "vector"])
         round_w1(1, 0, 1, ["scalar", "scalar"])
+        quantize_w1([1], 0, 0)
+        quantize_w1([1], 0, 1)
 
         top_slope = []
         for lo, hi in [(0, last), (last, n_tiles)]:
             pairs = held([P, hi - lo, 2], F32, "top_slope%d" % lo)
             nc.vector.scalar_tensor_tensor(
                 out=pairs[:, :, 1],
-                in0=sharp_t[:].rearrange("p b i -> p (b i)")[:, lo:hi],
+                in0=sharp_t.rearrange("p b i -> p (b i)")[:, lo:hi],
                 scalar=-1.0,
-                in1=share_t[:].rearrange("p b i -> p (b i)")[:, lo:hi],
+                in1=share_t.rearrange("p b i -> p (b i)")[:, lo:hi],
                 op0=ALU.mult,
                 op1=ALU.mult,
             )
@@ -270,7 +278,7 @@ def tile_list_bed_echo_marker_kernel(
                 e_w[b, start // HALF] = words[:, start - lo : start - lo + HALF]
                 e_s[b, start // HALF] = planes[:, start - lo : start - lo + HALF]
 
-        y = {(u, g): y_pool.tile([P, 2, HALF], F32, name="y%d%d" % (u, g)) for u in range(2) for g in range(2)}
+        y = {(u, g): y_pool.tile([P, 2, HALF], F32, name="y%d%d" % (u, g), tag="y%d%d" % (u, g)) for u in range(2) for g in range(2)}
 
         def score(b, u):
             for c in range(N // P):
@@ -286,46 +294,28 @@ def tile_list_bed_echo_marker_kernel(
                 )
 
         def finish(u, g, engine):
-            res = held([P, 2, HALF], F32, "res%d%d" % (u, g))
-            if engine == "gpsimd":
-                sums = held([P, 2, HALF], F32, "sums%d%d" % (u, g), "h%d" % (2 * u + g))
-                nc.scalar.copy(out=sums[:], in_=y[u, g][:])
             for within in range(2):
                 c = 2 * g + within
-                if engine == "gpsimd":
-                    nc.gpsimd.tensor_scalar(
-                        out=res[:, within, :],
-                        in0=sums[:, within, :],
-                        scalar1=3.0e38,
-                        scalar2=mark_t[:, c : c + 1],
-                        op0=ALU.min,
-                        op1=ALU.max,
-                    )
-                else:
-                    nc.vector.tensor_scalar(
-                        out=res[:, within, :],
-                        in0=y[u, g][:, within, :],
-                        scalar1=mark_t[:, c : c + 1],
-                        scalar2=None,
-                        op0=ALU.max,
-                    )
-            rows = out[2 * P * g : 2 * P * (g + 1), HALF * u : HALF * (u + 1)]
-            nc.sync.dma_start(out=rows.rearrange("(c p) m -> p c m", p=P), in_=res[:])
+                res = held([P, HALF], F32, "res%d%d" % (u, c))
+                nc.vector.tensor_scalar(
+                    out=res[:], in0=y[u, g][:, within, :], scalar1=mark_t[:, c : c + 1], scalar2=None, op0=ALU.max
+                )
+                nc.sync.dma_start(out=out[P * c : P * (c + 1), HALF * u : HALF * (u + 1)], in_=res[:])
 
         whole = [(0, M)]
         halves = [(0, HALF), (HALF, M)]
         for t in range(n_tiles):
             make_h(t)
             look(t, halves if t == last else whole)
-            if t == 0:
-                quantize_w1([0, 1], 0, 1, "firn0")
+            if t == 1:
                 round_w1(0, 1, 0, ["vector"])
+            if t == 1:
                 round_w1(1, 1, 0, ["vector"])
                 quantize_w1([0, 1], 1, 0)
                 round_w1(0, 1, 1, ["scalar"])
                 round_w1(1, 1, 1, ["scalar"])
-            if t == 3:
-                quantize_w1([0, 1], 1, 1, "firn3")
+            if t == 4:
+                quantize_w1([0, 1], 1, 1, "firn4")
         e_rows[0] = held([P, PACK, M], BF16, "e_rows0")
         for t in range(PACK):
             make_e_gpsimd(t, "w1_bf10")
@@ -342,7 +332,7 @@ def tile_list_bed_echo_marker_kernel(
         weave_e(1, 0, HALF, "vector")
         make_e(last, HALF, M)
         quantize_e(1, 0, HALF)
-        weave_e(1, HALF, M, "vector")
+        weave_e(1, HALF, M, "scalar")
         score(1, 0)
         quantize_e(1, HALF, M)
         finish(0, 0, "vector")

@@ -23,6 +23,12 @@ PACK = 4
 PASS = P * PACK
 BANK = 512
 HALF = M // 2
+PER_COLUMN = 16
+QUADRANT = 32
+ACC_BANKS = 4
+MARK_ROW = 8
+LATE_W1_TILE = 1
+LAST_PAIR_TILE = 4
 
 
 def tile_list_bed_echo_marker_kernel(
@@ -34,14 +40,14 @@ def tile_list_bed_echo_marker_kernel(
 
     with ExitStack() as ctx:
         keep = ctx.enter_context(tc.tile_pool(name="keep", bufs=1))
-        acc_pool = ctx.enter_context(tc.psum_pool(name="acc", bufs=4))
+        acc_pool = ctx.enter_context(tc.psum_pool(name="acc", bufs=ACC_BANKS))
         y_pool = ctx.enter_context(tc.psum_pool(name="y", bufs=1))
 
-        def held(shape, dtype, name, tag=None):
-            return keep.tile(shape, dtype, name=name, tag=tag or name, align_bytes=64)
+        def held(shape, dtype, name, over=None):
+            return keep.tile(shape, dtype, name=name, tag=over or name, align_bytes=64)
 
-        trace_list = held([P, S // 16], U16, "trace_list")
-        arm_lists = held([P, M // 16], U16, "arm_lists")
+        trace_list = held([P, S // PER_COLUMN], U16, "trace_list")
+        arm_lists = held([P, M // PER_COLUMN], U16, "arm_lists")
         tab_w = [held([P, T], I32, "tab_w%d" % a) for a in range(2)]
         tab_s = held([P, T], U8, "tab_s")
         firn_t = [held([P, S], F32, "firn%d" % t) for t in range(n_tiles)]
@@ -71,28 +77,29 @@ def tile_list_bed_echo_marker_kernel(
         nc.gpsimd.memset(w2_s[:].rearrange("p a n -> p (a n)").bitcast(I32), 0)
         nc.sync.dma_start(out=trace_list[:], in_=offs)
         nc.sync.dma_start(out=arm_lists[:], in_=offs2)
-        for q in range(4):
+        for q in range(P // QUADRANT):
             nc.sync.dma_start(
-                out=tab_s[32 * q : 32 * q + 8, :].bitcast(I32), in_=tab_scales[:, 4 * q : 4 * q + 4, :].bitcast(I32)
+                out=tab_s[QUADRANT * q : QUADRANT * q + 8, :].bitcast(I32),
+                in_=tab_scales[:, 4 * q : 4 * q + 4, :].bitcast(I32),
             )
         load_words(0)
         load_words(1)
         for row, vec in enumerate([level, sharp, share, gain]):
             nc.sync.dma_start(out=vec_rows[2 * row : 2 * row + 2, :], in_=vec.rearrange("(b c) -> b c", b=2))
-        nc.sync.dma_start(out=vec_rows[8:9, :], in_=mark.rearrange("(b c) -> b c", b=1))
+        nc.sync.dma_start(out=vec_rows[MARK_ROW : MARK_ROW + 1, :], in_=mark.rearrange("(b c) -> b c", b=1))
         load_w1(0, 0, 0, P)
         load_w1(1, 0, 0, P // 2)
         load_w1(1, 0, P // 2, P)
-        load_firn(0)
-        load_firn(1)
+        for t in range(LATE_W1_TILE + 1):
+            load_firn(t)
         load_w1(0, 1, 0, P)
         load_w1(1, 1, 0, P)
-        for t in range(2, n_tiles):
+        for t in range(LATE_W1_TILE + 1, n_tiles):
             load_firn(t)
         nc.sync.dma_start(out=w2_w[:].bitcast(I32), in_=w2_words.rearrange("a p n -> p a n").bitcast(I32))
-        for q in range(4):
+        for q in range(P // QUADRANT):
             nc.sync.dma_start(
-                out=w2_s[32 * q : 32 * q + 4, :, :].bitcast(I32),
+                out=w2_s[QUADRANT * q : QUADRANT * q + 4, :, :].bitcast(I32),
                 in_=w2_scales[:, 4 * q : 4 * q + 4, :].rearrange("a r n -> r a n").bitcast(I32),
             )
 
@@ -104,94 +111,86 @@ def tile_list_bed_echo_marker_kernel(
             nc.tensor.transpose(out=turned[:, i, :], in_=vec_rows[:, i:PASS:PACK], identity=identity[:])
         for c in range(N // P):
             nc.tensor.transpose(out=turned_mark[:, c, :], in_=vec_rows[:, P * c : P * (c + 1)], identity=identity[:])
-        nc.scalar.copy(out=by_row[:].rearrange("p v b i -> p (v b) i"), in_=turned[:, :, 0:8].rearrange("p i k -> p k i"))
-        nc.scalar.copy(out=mark_t[:], in_=turned_mark[:, :, 8])
+        nc.scalar.copy(
+            out=by_row[:].rearrange("p v b i -> p (v b) i"), in_=turned[:, :, 0:MARK_ROW].rearrange("p i k -> p k i")
+        )
+        nc.scalar.copy(out=mark_t[:], in_=turned_mark[:, :, MARK_ROW])
         level_t, sharp_t, share_t, gain_t = [by_row[:, v, :, :] for v in range(4)]
+
+        warm = held([P, 1], F32, "warm")
+        nc.scalar.activation(out=warm[:], in_=identity[:, 0:1], func=ACT.Sigmoid)
 
         v_s = held([P, S], U8, "v_s")
         v_w = {(a, u): held([P, BANK], U32, "v_w%d%d" % (a, u)) for a in range(2) for u in range(2)}
 
         def gather_words(a):
             for u in range(2):
-                cols = trace_list[:, 32 * u : 32 * (u + 1)]
-                nc.vector.tensor_copy(out=v_w[a, u][:], in_=tab_w[a][:].bitcast(U32).indirect(cols))
+                entries = trace_list[:, BANK // PER_COLUMN * u : BANK // PER_COLUMN * (u + 1)]
+                nc.vector.tensor_copy(out=v_w[a, u][:], in_=tab_w[a][:].bitcast(U32).indirect(entries))
 
         w1_bf = {}
         w1_w = {}
         w1_s = {}
 
-        def round_w1(a, b, pair, engines, tag=None):
+        def round_w1(a, b, pair):
             if a == 0:
-                w1_bf[b, pair] = held([P, 2, 2, P, PACK], BF16, "w1_bf%d%d" % (b, pair), tag)
-            for (lo, hi, raw), engine in zip(w1_raw[a, b], engines):
-                src = raw[:].rearrange("p j (m t) -> p m j t", t=PACK)[:, :, :, 2 * pair : 2 * pair + 2]
-                dst = w1_bf[b, pair][:, a, :, lo:hi, :].rearrange("p t m j -> p m j t")
-                if engine == "scalar":
-                    nc.scalar.copy(out=dst, in_=src)
-                elif engine == "gpsimd":
-                    nc.gpsimd.tensor_scalar(
-                        out=dst.rearrange("p m j t -> p m t j"),
-                        in0=src.rearrange("p m j t -> p m t j"),
-                        scalar1=1.0,
-                        scalar2=1.0,
-                        op0=ALU.mult,
-                        op1=ALU.mult,
-                    )
-                else:
+                w1_bf[b, pair] = held([P, 2, 2, P, PACK], BF16, "w1_bf%d%d" % (b, pair))
+            for lo, hi, raw in w1_raw[a, b]:
+                src = raw[:].rearrange("p j (m i) -> p m j i", i=PACK)[:, :, :, 2 * pair : 2 * pair + 2]
+                dst = w1_bf[b, pair][:, a, :, lo:hi, :].rearrange("p s m j -> p m j s")
+                if pair == 0:
                     nc.vector.tensor_copy(out=dst, in_=src)
+                else:
+                    nc.scalar.copy(out=dst, in_=src)
 
-        def quantize_w1(passes, b, pair, tag=None):
+        def quantize_w1(passes, b, pair, over=None):
             first, count = passes[0], len(passes)
-            words = held([P, 2 * P * count], U32, "w1_w%d%d%d" % (first, b, pair), tag)
-            planes = held([P, 2 * P * count], U8, "w1_s%d%d%d" % (first, b, pair))
+            words = held([P, 2 * P * count], U32, "w1_w%d%d%d" % (first, b, pair), over)
+            scales = held([P, 2 * P * count], U8, "w1_s%d%d%d" % (first, b, pair))
             nc.vector.quantize_mx(
                 out=words[:].bitcast(FP8X4),
-                scales=planes[:],
-                in_=w1_bf[b, pair][:, first : first + count, :, :, :].rearrange("p a t m j -> p (a t m j)"),
+                scales=scales[:],
+                in_=w1_bf[b, pair][:, first : first + count, :, :, :].rearrange("p a s m j -> p (a s m j)"),
             )
             for a in passes:
                 w1_w[a, b, pair] = words[:, 2 * P * (a - first) : 2 * P * (a - first + 1)]
-                w1_s[a, b, pair] = planes[:, 2 * P * (a - first) : 2 * P * (a - first + 1)]
+                w1_s[a, b, pair] = scales[:, 2 * P * (a - first) : 2 * P * (a - first + 1)]
 
         nc.vector.tensor_copy(out=v_s[:], in_=tab_s[:].indirect(trace_list[:]))
         gather_words(0)
         gather_words(1)
-        round_w1(0, 0, 0, ["vector"])
-        round_w1(0, 0, 1, ["scalar"])
-        quantize_w1([0], 0, 0)
-        quantize_w1([0], 0, 1)
-        round_w1(1, 0, 0, ["vector", "vector"])
-        round_w1(1, 0, 1, ["scalar", "scalar"])
-        quantize_w1([1], 0, 0)
-        quantize_w1([1], 0, 1)
+        for a in range(2):
+            round_w1(a, 0, 0)
+            round_w1(a, 0, 1)
+            quantize_w1([a], 0, 0)
+            quantize_w1([a], 0, 1)
 
         top_slope = []
         for lo, hi in [(0, last), (last, n_tiles)]:
-            pairs = held([P, hi - lo, 2], F32, "top_slope%d" % lo)
+            both = held([P, hi - lo, 2], F32, "top_slope%d" % lo)
             nc.vector.scalar_tensor_tensor(
-                out=pairs[:, :, 1],
+                out=both[:, :, 1],
                 in0=sharp_t.rearrange("p b i -> p (b i)")[:, lo:hi],
                 scalar=-1.0,
                 in1=share_t.rearrange("p b i -> p (b i)")[:, lo:hi],
                 op0=ALU.mult,
                 op1=ALU.mult,
             )
-            top_slope.extend(pairs[:, t, :] for t in range(hi - lo))
+            top_slope.extend(both[:, t, :] for t in range(hi - lo))
 
         h = [held([P, S], F32, "h%d" % t) for t in range(n_tiles)]
         shift = held([P, n_tiles], F32, "shift")
         picked = [held([P, M], F32, "picked%d" % t) for t in range(n_tiles)]
         gate = [held([P, M], F32, "gate%d" % t) for t in range(n_tiles)]
-        e_rows = {}
 
-        def column(tile, t):
+        def column(vector_t, t):
             b, i = divmod(t, PACK)
-            return tile[:, b, i : i + 1]
+            return vector_t[:, b, i : i + 1]
 
         def make_h(t):
             b, i = divmod(t, PACK)
-            pair, within = divmod(i, 2)
-            cols = slice(P * within, P * (within + 1))
+            pair, s = divmod(i, 2)
+            cols = slice(P * s, P * (s + 1))
             for u in range(2):
                 acc = acc_pool.tile([P, BANK], F32, name="acc")
                 for a in range(2):
@@ -220,16 +219,92 @@ def tile_list_bed_echo_marker_kernel(
             for lo, hi in spans:
                 nc.scalar.activation(
                     out=gate[t][:, lo:hi],
-                    in_=h[t][:].indirect(arm_lists[:, lo // 16 : hi // 16]),
+                    in_=h[t][:].indirect(arm_lists[:, lo // PER_COLUMN : hi // PER_COLUMN]),
                     func=ACT.Sigmoid,
                     bias=shift[:, t : t + 1],
                     scale=column(sharp_t, t),
                 )
 
+        y = {
+            (u, g): y_pool.tile([P, 2, HALF], F32, name="y%d%d" % (u, g), tag="y%d%d" % (u, g))
+            for u in range(2)
+            for g in range(2)
+        }
+
+        for t in range(n_tiles):
+            make_h(t)
+            look(t, [(0, HALF), (HALF, M)] if t == last else [(0, M)])
+            if t == LATE_W1_TILE:
+                round_w1(0, 1, 0)
+                round_w1(1, 1, 0)
+                quantize_w1([0, 1], 1, 0)
+                round_w1(0, 1, 1)
+                round_w1(1, 1, 1)
+            if t == LAST_PAIR_TILE:
+                quantize_w1([0, 1], 1, 1, over="firn%d" % t)
+
+        e_rows = {}
+        e_bf = {}
+        e_w = {}
+        e_s = {}
+
+        def quantize_e(b, lo, hi, over=None):
+            words = held([P, hi - lo], U32, "e_w%d%d" % (b, lo), over)
+            scales = held([P, hi - lo], U8, "e_s%d%d" % (b, lo))
+            nc.vector.quantize_mx(
+                out=words[:].bitcast(FP8X4), scales=scales[:], in_=e_bf[b, lo][:].rearrange("p m i -> p (m i)")
+            )
+            for start in range(lo, hi, HALF):
+                e_w[b, start // HALF] = words[:, start - lo : start - lo + HALF]
+                e_s[b, start // HALF] = scales[:, start - lo : start - lo + HALF]
+
+        def score(b, u):
+            for c in range(N // P):
+                g, place = divmod(c, 2)
+                nc.tensor.matmul_mx(
+                    out=y[u, g][:, place, :],
+                    lhsT=w2_w[:, b, 2 * P * c : 2 * P * (c + 1)].bitcast(FP4X4),
+                    lhsT_scale=w2_s[:, b, P * c : P * (c + 1)],
+                    rhs=e_w[b, u].bitcast(FP8X4),
+                    rhs_scale=e_s[b, u],
+                    start=(b == 0 and place == 0),
+                    stop=(b == 1 and place == 1),
+                )
+
+        def finish(u):
+            for c in range(N // P):
+                g, place = divmod(c, 2)
+                res = held([P, HALF], F32, "res%d%d" % (u, c))
+                nc.vector.tensor_scalar(
+                    out=res[:], in0=y[u, g][:, place, :], scalar1=mark_t[:, c : c + 1], scalar2=None, op0=ALU.max
+                )
+                nc.sync.dma_start(out=out[P * c : P * (c + 1), HALF * u : HALF * (u + 1)], in_=res[:])
+
+        e_rows[0] = held([P, PACK, M], BF16, "e_rows0")
+        for t in range(PACK):
+            scaled = held([P, M], F32, "scaled%d" % t, over="w1_bf10")
+            nc.gpsimd.tensor_scalar(
+                out=scaled[:], in0=picked[t][:], scalar1=column(gain_t, t), scalar2=1.0, op0=ALU.mult, op1=ALU.mult
+            )
+            nc.gpsimd.tensor_tensor(out=e_rows[0][:, t, :], in0=scaled[:], in1=gate[t][:], op=ALU.mult)
+        e_bf[0, 0] = held([P, M, PACK], BF16, "e_bf00")
+        nc.gpsimd.tensor_scalar(
+            out=e_bf[0, 0][:],
+            in0=e_rows[0][:].rearrange("p i m -> p m i"),
+            scalar1=1.0,
+            scalar2=1.0,
+            op0=ALU.mult,
+            op1=ALU.mult,
+        )
+
+        e_rows[1] = held([P, PACK, M], BF16, "e_rows1", over="firn%d" % last)
+        quantize_e(0, 0, M, over="top_slope%d" % last)
+        score(0, 0)
+        score(0, 1)
+
         def make_e(t, lo, hi):
-            b, i = divmod(t, PACK)
             nc.vector.scalar_tensor_tensor(
-                out=e_rows[b][:, i, lo:hi],
+                out=e_rows[1][:, t - PACK, lo:hi],
                 in0=picked[t][:, lo:hi],
                 scalar=column(gain_t, t),
                 in1=gate[t][:, lo:hi],
@@ -237,106 +312,23 @@ def tile_list_bed_echo_marker_kernel(
                 op1=ALU.mult,
             )
 
-        def make_e_gpsimd(t, tag):
-            b, i = divmod(t, PACK)
-            scaled = held([P, M], F32, "scaled%d" % t, tag)
-            nc.gpsimd.tensor_scalar(
-                out=scaled[:], in0=picked[t][:], scalar1=column(gain_t, t), scalar2=1.0, op0=ALU.mult, op1=ALU.mult
-            )
-            nc.gpsimd.tensor_tensor(out=e_rows[b][:, i, :], in0=scaled[:], in1=gate[t][:], op=ALU.mult)
+        def weave_views(lo, hi):
+            e_bf[1, lo] = held([P, hi - lo, PACK], BF16, "e_bf%d%d" % (1, lo))
+            dst = e_bf[1, lo][:].rearrange("p (c q) i -> p c i q", q=4)
+            src = e_rows[1][:, :, lo:hi].rearrange("p i (c q) -> p c i q", q=4)
+            return dst, src
 
-        e_bf = {}
-        e_w = {}
-        e_s = {}
-
-        def weave_e(b, lo, hi, engine, tag=None):
-            e_bf[b, lo] = held([P, hi - lo, PACK], BF16, "e_bf%d%d" % (b, lo), tag)
-            if engine == "gpsimd":
-                nc.gpsimd.tensor_scalar(
-                    out=e_bf[b, lo][:],
-                    in0=e_rows[b][:, :, lo:hi].rearrange("p i m -> p m i"),
-                    scalar1=1.0,
-                    scalar2=1.0,
-                    op0=ALU.mult,
-                    op1=ALU.mult,
-                )
-            else:
-                dst = e_bf[b, lo][:].rearrange("p (c q) i -> p c i q", q=4)
-                src = e_rows[b][:, :, lo:hi].rearrange("p i (c q) -> p c i q", q=4)
-                if engine == "scalar":
-                    nc.scalar.copy(out=dst, in_=src)
-                else:
-                    nc.vector.tensor_copy(out=dst, in_=src)
-
-        def quantize_e(b, lo, hi, tag=None):
-            words = held([P, hi - lo], U32, "e_w%d%d" % (b, lo), tag)
-            planes = held([P, hi - lo], U8, "e_s%d%d" % (b, lo))
-            nc.vector.quantize_mx(
-                out=words[:].bitcast(FP8X4), scales=planes[:], in_=e_bf[b, lo][:].rearrange("p m i -> p (m i)")
-            )
-            for start in range(lo, hi, HALF):
-                e_w[b, start // HALF] = words[:, start - lo : start - lo + HALF]
-                e_s[b, start // HALF] = planes[:, start - lo : start - lo + HALF]
-
-        y = {(u, g): y_pool.tile([P, 2, HALF], F32, name="y%d%d" % (u, g), tag="y%d%d" % (u, g)) for u in range(2) for g in range(2)}
-
-        def score(b, u):
-            for c in range(N // P):
-                g, within = divmod(c, 2)
-                nc.tensor.matmul_mx(
-                    out=y[u, g][:, within, :],
-                    lhsT=w2_w[:, b, 2 * P * c : 2 * P * (c + 1)].bitcast(FP4X4),
-                    lhsT_scale=w2_s[:, b, P * c : P * (c + 1)],
-                    rhs=e_w[b, u].bitcast(FP8X4),
-                    rhs_scale=e_s[b, u],
-                    start=(b == 0 and within == 0),
-                    stop=(b == 1 and within == 1),
-                )
-
-        def finish(u, g, engine):
-            for within in range(2):
-                c = 2 * g + within
-                res = held([P, HALF], F32, "res%d%d" % (u, c))
-                nc.vector.tensor_scalar(
-                    out=res[:], in0=y[u, g][:, within, :], scalar1=mark_t[:, c : c + 1], scalar2=None, op0=ALU.max
-                )
-                nc.sync.dma_start(out=out[P * c : P * (c + 1), HALF * u : HALF * (u + 1)], in_=res[:])
-
-        whole = [(0, M)]
-        halves = [(0, HALF), (HALF, M)]
-        for t in range(n_tiles):
-            make_h(t)
-            look(t, halves if t == last else whole)
-            if t == 1:
-                round_w1(0, 1, 0, ["vector"])
-            if t == 1:
-                round_w1(1, 1, 0, ["vector"])
-                quantize_w1([0, 1], 1, 0)
-                round_w1(0, 1, 1, ["scalar"])
-                round_w1(1, 1, 1, ["scalar"])
-            if t == 4:
-                quantize_w1([0, 1], 1, 1, "firn4")
-        e_rows[0] = held([P, PACK, M], BF16, "e_rows0")
-        for t in range(PACK):
-            make_e_gpsimd(t, "w1_bf10")
-        weave_e(0, 0, M, "gpsimd")
-        e_rows[1] = held([P, PACK, M], BF16, "e_rows1", "firn7")
-        for t in range(PACK, 4):
-            make_e_gpsimd(t, "w1_bf10")
-        quantize_e(0, 0, M, "top_slope7")
-        score(0, 0)
-        score(0, 1)
-        for t in range(4, last):
+        for t in range(PACK, last):
             make_e(t, 0, M)
         make_e(last, 0, HALF)
-        weave_e(1, 0, HALF, "vector")
+        dst, src = weave_views(0, HALF)
+        nc.vector.tensor_copy(out=dst, in_=src)
         make_e(last, HALF, M)
         quantize_e(1, 0, HALF)
-        weave_e(1, HALF, M, "scalar")
+        dst, src = weave_views(HALF, M)
+        nc.scalar.copy(out=dst, in_=src)
         score(1, 0)
         quantize_e(1, HALF, M)
-        finish(0, 0, "vector")
-        finish(0, 1, "vector")
+        finish(0)
         score(1, 1)
-        finish(1, 0, "vector")
-        finish(1, 1, "vector")
+        finish(1)

from contextlib import ExitStack

import concourse.mybir as mybir
from concourse.masks import make_identity

K, T, S, H, M, N = 1024, 2048, 1024, 1024, 512, 512
FLOPS = 2 * K * H * S + 2 * H * N * M

F32 = mybir.dt.float32
BF16 = mybir.dt.bfloat16
I32 = mybir.dt.int32
U32 = mybir.dt.uint32
U16 = mybir.dt.uint16
U8 = mybir.dt.uint8
FP8X4 = mybir.dt.float8_e4m3fn_x4
FP4X4 = mybir.dt.float4_e2m1fn_x4
ALU = mybir.AluOpType
ACT = mybir.ActivationFunctionType
AXIS = mybir.AxisListType

P = 128
PACK = 4
PASS = P * PACK
BANK = 512
HALF = M // 2
PER_COLUMN = 16
QUADRANT = 32
ACC_BANKS = 4
MARK_ROW = 8
LATE_W1_TILE = 1
LAST_PAIR_TILE = 4


def tile_list_bed_echo_marker_kernel(
    tc, tab_words, tab_scales, offs, offs2, w1, level, firn, sharp, share, gain, w2_words, w2_scales, mark, out
):
    nc = tc.nc
    n_tiles = H // P
    last = n_tiles - 1

    with ExitStack() as ctx:
        keep = ctx.enter_context(tc.tile_pool(name="keep", bufs=1))
        acc_pool = ctx.enter_context(tc.psum_pool(name="acc", bufs=ACC_BANKS))
        y_pool = ctx.enter_context(tc.psum_pool(name="y", bufs=1))

        def held(shape, dtype, name, over=None):
            return keep.tile(shape, dtype, name=name, tag=over or name, align_bytes=64)

        trace_list = held([P, S // PER_COLUMN], U16, "trace_list")
        arm_lists = held([P, M // PER_COLUMN], U16, "arm_lists")
        tab_w = [held([P, T], I32, "tab_w%d" % a) for a in range(2)]
        tab_s = held([P, T], U8, "tab_s")
        firn_t = [held([P, S], F32, "firn%d" % t) for t in range(n_tiles)]
        vec_rows = held([P, PASS], F32, "vec_rows")
        identity = held([P, P], F32, "identity")
        w2_w = held([P, 2, 2 * N], U8, "w2_w")
        w2_s = held([P, 2, N], U8, "w2_s")
        w1_raw = {}

        def load_w1(a, b, lo, hi):
            raw = held([P, PACK, PACK * (hi - lo)], F32, "w1_raw%d%d_%d" % (a, b, lo))
            rows = w1[PASS * a : PASS * (a + 1), PASS * b + PACK * lo : PASS * b + PACK * hi]
            nc.sync.dma_start(out=raw[:], in_=rows.rearrange("(p j) c -> p j c", j=PACK))
            w1_raw.setdefault((a, b), []).append((lo, hi, raw))

        def load_firn(t):
            b, i = divmod(t, PACK)
            rows = firn[PASS * b : PASS * (b + 1), :].rearrange("(p i) j -> p i j", i=PACK)
            nc.sync.dma_start(out=firn_t[t][:], in_=rows[:, i, :])

        def load_words(a):
            nc.sync.dma_start(out=tab_w[a][:], in_=tab_words[a].rearrange("p t i -> p (t i)").bitcast(I32))

        nc.gpsimd.memset(tab_s[:].bitcast(I32), 0)
        nc.gpsimd.memset(vec_rows[:], 0.0)
        make_identity(nc, identity[:])
        nc.gpsimd.memset(w2_s[:].rearrange("p a n -> p (a n)").bitcast(I32), 0)
        nc.sync.dma_start(out=trace_list[:], in_=offs)
        nc.sync.dma_start(out=arm_lists[:], in_=offs2)
        for q in range(P // QUADRANT):
            nc.sync.dma_start(
                out=tab_s[QUADRANT * q : QUADRANT * q + 8, :].bitcast(I32),
                in_=tab_scales[:, 4 * q : 4 * q + 4, :].bitcast(I32),
            )
        load_words(0)
        load_words(1)
        for row, vec in enumerate([level, sharp, share, gain]):
            nc.sync.dma_start(out=vec_rows[2 * row : 2 * row + 2, :], in_=vec.rearrange("(b c) -> b c", b=2))
        nc.sync.dma_start(out=vec_rows[MARK_ROW : MARK_ROW + 1, :], in_=mark.rearrange("(b c) -> b c", b=1))
        load_w1(0, 0, 0, P)
        load_w1(1, 0, 0, P // 2)
        load_w1(1, 0, P // 2, P)
        for t in range(LATE_W1_TILE + 1):
            load_firn(t)
        load_w1(0, 1, 0, P)
        load_w1(1, 1, 0, P)
        for t in range(LATE_W1_TILE + 1, n_tiles):
            load_firn(t)
        nc.sync.dma_start(out=w2_w[:].bitcast(I32), in_=w2_words.rearrange("a p n -> p a n").bitcast(I32))
        for q in range(P // QUADRANT):
            nc.sync.dma_start(
                out=w2_s[QUADRANT * q : QUADRANT * q + 4, :, :].bitcast(I32),
                in_=w2_scales[:, 4 * q : 4 * q + 4, :].rearrange("a r n -> r a n").bitcast(I32),
            )

        by_row = held([P, 4, 2, PACK], F32, "by_row")
        mark_t = held([P, N // P], F32, "mark_t")
        turned = y_pool.tile([P, PACK, P], F32, name="turned", tag="y00")
        turned_mark = y_pool.tile([P, N // P, P], F32, name="turned_mark", tag="y01")
        for i in range(PACK):
            nc.tensor.transpose(out=turned[:, i, :], in_=vec_rows[:, i:PASS:PACK], identity=identity[:])
        for c in range(N // P):
            nc.tensor.transpose(out=turned_mark[:, c, :], in_=vec_rows[:, P * c : P * (c + 1)], identity=identity[:])
        nc.scalar.copy(
            out=by_row[:].rearrange("p v b i -> p (v b) i"), in_=turned[:, :, 0:MARK_ROW].rearrange("p i k -> p k i")
        )
        nc.scalar.copy(out=mark_t[:], in_=turned_mark[:, :, MARK_ROW])
        level_t, sharp_t, share_t, gain_t = [by_row[:, v, :, :] for v in range(4)]

        warm = held([P, 1], F32, "warm")
        nc.scalar.activation(out=warm[:], in_=identity[:, 0:1], func=ACT.Sigmoid)

        v_s = held([P, S], U8, "v_s")
        v_w = {(a, u): held([P, BANK], U32, "v_w%d%d" % (a, u)) for a in range(2) for u in range(2)}

        def gather_words(a):
            for u in range(2):
                entries = trace_list[:, BANK // PER_COLUMN * u : BANK // PER_COLUMN * (u + 1)]
                nc.vector.tensor_copy(out=v_w[a, u][:], in_=tab_w[a][:].bitcast(U32).indirect(entries))

        w1_bf = {}
        w1_w = {}
        w1_s = {}

        def round_w1(a, b, pair):
            if a == 0:
                w1_bf[b, pair] = held([P, 2, 2, P, PACK], BF16, "w1_bf%d%d" % (b, pair))
            for lo, hi, raw in w1_raw[a, b]:
                src = raw[:].rearrange("p j (m i) -> p m j i", i=PACK)[:, :, :, 2 * pair : 2 * pair + 2]
                dst = w1_bf[b, pair][:, a, :, lo:hi, :].rearrange("p s m j -> p m j s")
                if pair == 0:
                    nc.vector.tensor_copy(out=dst, in_=src)
                else:
                    nc.scalar.copy(out=dst, in_=src)

        def quantize_w1(passes, b, pair, over=None):
            first, count = passes[0], len(passes)
            words = held([P, 2 * P * count], U32, "w1_w%d%d%d" % (first, b, pair), over)
            scales = held([P, 2 * P * count], U8, "w1_s%d%d%d" % (first, b, pair))
            nc.vector.quantize_mx(
                out=words[:].bitcast(FP8X4),
                scales=scales[:],
                in_=w1_bf[b, pair][:, first : first + count, :, :, :].rearrange("p a s m j -> p (a s m j)"),
            )
            for a in passes:
                w1_w[a, b, pair] = words[:, 2 * P * (a - first) : 2 * P * (a - first + 1)]
                w1_s[a, b, pair] = scales[:, 2 * P * (a - first) : 2 * P * (a - first + 1)]

        nc.vector.tensor_copy(out=v_s[:], in_=tab_s[:].indirect(trace_list[:]))
        gather_words(0)
        gather_words(1)
        for a in range(2):
            round_w1(a, 0, 0)
            round_w1(a, 0, 1)
            quantize_w1([a], 0, 0)
            quantize_w1([a], 0, 1)

        top_slope = []
        for lo, hi in [(0, last), (last, n_tiles)]:
            both = held([P, hi - lo, 2], F32, "top_slope%d" % lo)
            nc.vector.scalar_tensor_tensor(
                out=both[:, :, 1],
                in0=sharp_t.rearrange("p b i -> p (b i)")[:, lo:hi],
                scalar=-1.0,
                in1=share_t.rearrange("p b i -> p (b i)")[:, lo:hi],
                op0=ALU.mult,
                op1=ALU.mult,
            )
            top_slope.extend(both[:, t, :] for t in range(hi - lo))

        h = [held([P, S], F32, "h%d" % t) for t in range(n_tiles)]
        shift = held([P, n_tiles], F32, "shift")
        picked = [held([P, M], F32, "picked%d" % t) for t in range(n_tiles)]
        gate = [held([P, M], F32, "gate%d" % t) for t in range(n_tiles)]

        def column(vector_t, t):
            b, i = divmod(t, PACK)
            return vector_t[:, b, i : i + 1]

        def make_h(t):
            b, i = divmod(t, PACK)
            pair, s = divmod(i, 2)
            cols = slice(P * s, P * (s + 1))
            for u in range(2):
                acc = acc_pool.tile([P, BANK], F32, name="acc")
                for a in range(2):
                    nc.tensor.matmul_mx(
                        out=acc[:],
                        lhsT=w1_w[a, b, pair][:, cols].bitcast(FP8X4),
                        lhsT_scale=w1_s[a, b, pair][:, cols],
                        rhs=v_w[a, u][:].bitcast(FP8X4),
                        rhs_scale=v_s[4 * a : P, BANK * u : BANK * (u + 1)],
                        start=(a == 0),
                        stop=(a == 1),
                    )
                nc.vector.scalar_tensor_tensor(
                    out=h[t][:, BANK * u : BANK * (u + 1)],
                    in0=acc[:],
                    scalar=column(level_t, t),
                    in1=firn_t[t][:, BANK * u : BANK * (u + 1)],
                    op0=ALU.mult,
                    op1=ALU.add,
                )

        def look(t, spans):
            nc.vector.tensor_reduce(out=top_slope[t][:, 0:1], in_=h[t][:], axis=AXIS.X, op=ALU.max)
            nc.scalar.activation(out=picked[t][:], in_=h[t][:].indirect(arm_lists[:]), func=ACT.Copy)
            nc.vector.tensor_reduce(out=shift[:, t : t + 1], in_=top_slope[t], axis=AXIS.X, op=ALU.mult)
            for lo, hi in spans:
                nc.scalar.activation(
                    out=gate[t][:, lo:hi],
                    in_=h[t][:].indirect(arm_lists[:, lo // PER_COLUMN : hi // PER_COLUMN]),
                    func=ACT.Sigmoid,
                    bias=shift[:, t : t + 1],
                    scale=column(sharp_t, t),
                )

        y = {
            (u, g): y_pool.tile([P, 2, HALF], F32, name="y%d%d" % (u, g), tag="y%d%d" % (u, g))
            for u in range(2)
            for g in range(2)
        }

        for t in range(n_tiles):
            make_h(t)
            look(t, [(0, HALF), (HALF, M)] if t == last else [(0, M)])
            if t == LATE_W1_TILE:
                round_w1(0, 1, 0)
                round_w1(1, 1, 0)
                quantize_w1([0, 1], 1, 0)
                round_w1(0, 1, 1)
                round_w1(1, 1, 1)
            if t == LAST_PAIR_TILE:
                quantize_w1([0, 1], 1, 1, over="firn%d" % t)

        e_rows = {}
        e_bf = {}
        e_w = {}
        e_s = {}

        def quantize_e(b, lo, hi, over=None):
            words = held([P, hi - lo], U32, "e_w%d%d" % (b, lo), over)
            scales = held([P, hi - lo], U8, "e_s%d%d" % (b, lo))
            nc.vector.quantize_mx(
                out=words[:].bitcast(FP8X4), scales=scales[:], in_=e_bf[b, lo][:].rearrange("p m i -> p (m i)")
            )
            for start in range(lo, hi, HALF):
                e_w[b, start // HALF] = words[:, start - lo : start - lo + HALF]
                e_s[b, start // HALF] = scales[:, start - lo : start - lo + HALF]

        def score(b, u):
            for c in range(N // P):
                g, place = divmod(c, 2)
                nc.tensor.matmul_mx(
                    out=y[u, g][:, place, :],
                    lhsT=w2_w[:, b, 2 * P * c : 2 * P * (c + 1)].bitcast(FP4X4),
                    lhsT_scale=w2_s[:, b, P * c : P * (c + 1)],
                    rhs=e_w[b, u].bitcast(FP8X4),
                    rhs_scale=e_s[b, u],
                    start=(b == 0 and place == 0),
                    stop=(b == 1 and place == 1),
                )

        def finish(u):
            for c in range(N // P):
                g, place = divmod(c, 2)
                res = held([P, HALF], F32, "res%d%d" % (u, c))
                nc.vector.tensor_scalar(
                    out=res[:], in0=y[u, g][:, place, :], scalar1=mark_t[:, c : c + 1], scalar2=None, op0=ALU.max
                )
                nc.sync.dma_start(out=out[P * c : P * (c + 1), HALF * u : HALF * (u + 1)], in_=res[:])

        e_rows[0] = held([P, PACK, M], BF16, "e_rows0")
        for t in range(PACK):
            scaled = held([P, M], F32, "scaled%d" % t, over="w1_bf10")
            nc.gpsimd.tensor_scalar(
                out=scaled[:], in0=picked[t][:], scalar1=column(gain_t, t), scalar2=1.0, op0=ALU.mult, op1=ALU.mult
            )
            nc.gpsimd.tensor_tensor(out=e_rows[0][:, t, :], in0=scaled[:], in1=gate[t][:], op=ALU.mult)
        e_bf[0, 0] = held([P, M, PACK], BF16, "e_bf00")
        nc.gpsimd.tensor_scalar(
            out=e_bf[0, 0][:],
            in0=e_rows[0][:].rearrange("p i m -> p m i"),
            scalar1=1.0,
            scalar2=1.0,
            op0=ALU.mult,
            op1=ALU.mult,
        )

        e_rows[1] = held([P, PACK, M], BF16, "e_rows1", over="firn%d" % last)
        quantize_e(0, 0, M, over="top_slope%d" % last)
        score(0, 0)
        score(0, 1)

        def make_e(t, lo, hi):
            nc.vector.scalar_tensor_tensor(
                out=e_rows[1][:, t - PACK, lo:hi],
                in0=picked[t][:, lo:hi],
                scalar=column(gain_t, t),
                in1=gate[t][:, lo:hi],
                op0=ALU.mult,
                op1=ALU.mult,
            )

        def weave_views(lo, hi):
            e_bf[1, lo] = held([P, hi - lo, PACK], BF16, "e_bf%d%d" % (1, lo))
            dst = e_bf[1, lo][:].rearrange("p (c q) i -> p c i q", q=4)
            src = e_rows[1][:, :, lo:hi].rearrange("p i (c q) -> p c i q", q=4)
            return dst, src

        for t in range(PACK, last):
            make_e(t, 0, M)
        make_e(last, 0, HALF)
        dst, src = weave_views(0, HALF)
        nc.vector.tensor_copy(out=dst, in_=src)
        make_e(last, HALF, M)
        quantize_e(1, 0, HALF)
        dst, src = weave_views(HALF, M)
        nc.scalar.copy(out=dst, in_=src)
        score(1, 0)
        quantize_e(1, HALF, M)
        finish(0)
        score(1, 1)
        finish(1)
